import numpy as np
import ml_dtypes


def mxq(x, axis, fmt="e4m3"):
    dtype, down = {"e4m3": (ml_dtypes.float8_e4m3fn, 7), "e5m2": (ml_dtypes.float8_e5m2, 14)}[fmt]
    v = np.moveaxis(np.asarray(x, np.float32).astype(ml_dtypes.bfloat16).astype(np.float64), axis, -1)
    blocks = v.reshape(v.shape[:-1] + (-1, 32))
    amax = np.abs(blocks).max(-1, keepdims=True)
    byte = np.maximum(np.where(amax > 0, np.frexp(amax)[1] - 1 + 127, 0) - down, 1)
    scale = np.exp2(byte - 127.0)
    codes = (blocks / scale).astype(np.float32).astype(dtype).astype(np.float64)
    return np.moveaxis((codes * scale).reshape(v.shape), -1, axis)


WIDE = False


def mx_kscale(k):
    if not WIDE:
        return np.ones(k)
    levels = np.array([10, -10, 5, -5, 0])
    if k % 512:
        return np.exp2(np.random.permutation(np.resize(levels, k // 32))).repeat(32)
    a = np.empty((k // 512, 16))
    for p in range(k // 512):
        a[p, :8] = np.random.permutation(np.resize(levels, 8))
        for g in range(8):
            far = levels[np.abs(levels - a[p, g]) >= 10]
            a[p, g + 8] = far[np.random.randint(len(far))]
    return np.exp2(a.ravel()).repeat(32)


def f64(x):
    return np.asarray(x).astype(np.float64)


def striped8(idx):
    return np.concatenate([x.reshape(-1, 16).T for x in idx]).astype(np.uint16)


def runs(offs, k):
    lists = np.stack([offs[16 * r : 16 * r + 16].T.reshape(-1) for r in range(8)]).astype(np.int64)
    return lists[np.arange(k) % 512 // 64]


def pack_weight(w):
    k, n = w.shape
    w = f64(np.asarray(w, np.float32).astype(ml_dtypes.bfloat16)).reshape(k // 32, 32, n)
    amax = np.abs(w).max(1)
    byte = np.clip(np.where(amax > 0, np.frexp(amax)[1] - 1 + 127 - 7, 1), 1, 254)
    scaled = (w * np.exp2(127.0 - byte)[:, None, :]).reshape(k, n).astype(np.float32)
    words = np.ascontiguousarray(scaled.reshape(k // 512, 128, 4, n).transpose(0, 1, 3, 2)).astype(ml_dtypes.float8_e4m3fn).view(np.uint8)
    return words, np.ascontiguousarray(byte.astype(np.uint8).reshape(k // 512, 16, n))


def unpack_weight(words, scales):
    g, p, n, _ = words.shape
    vals = np.ascontiguousarray(words).view(ml_dtypes.float8_e4m3fn).astype(np.float64) * np.repeat(np.exp2(scales.astype(np.float64) - 127.0), 8, axis=1)[..., None]
    return vals.transpose(0, 1, 3, 2).reshape(g * 512, n)


E2M1 = np.array([0.0, 0.5, 1.0, 1.5, 2.0, 3.0, 4.0, 6.0, -0.0, -0.5, -1.0, -1.5, -2.0, -3.0, -4.0, -6.0])


def pack_fp4(w):
    k, n = w.shape
    w = f64(np.asarray(w, np.float32).astype(ml_dtypes.bfloat16)).reshape(k // 32, 32, n)
    amax = np.abs(w).max(1)
    mant, ex = np.frexp(amax / 6.0)
    byte = np.clip(np.where(amax > 0, np.where(mant > 0.5, ex, ex - 1) + 127, 1), 1, 254)
    scaled = (w * np.exp2(127.0 - byte)[:, None, :]).reshape(k, n).astype(np.float32)
    c = np.ascontiguousarray(scaled.reshape(k // 512, 128, 4, n).transpose(0, 1, 3, 2)).astype(ml_dtypes.float4_e2m1fn).view(np.uint8) & 0xF
    words = (c[..., 0::2] | (c[..., 1::2] << 4)).reshape(k // 512, 128, 2 * n)
    return np.ascontiguousarray(words), np.ascontiguousarray(byte.astype(np.uint8).reshape(k // 512, 16, n))


def unpack_fp4(words, scales):
    g, _, n = scales.shape
    words = np.ascontiguousarray(words).reshape(g, 128, n, 2)
    nib = np.empty((g, 128, n, 4), np.uint8)
    nib[..., 0::2] = words & 0xF
    nib[..., 1::2] = words >> 4
    vals = E2M1[nib] * np.repeat(np.exp2(scales.astype(np.float64) - 127.0), 8, axis=1)[..., None]
    return vals.transpose(0, 1, 3, 2).reshape(g * 512, n)


def planes(y):
    n, m = y.shape
    v = y.astype(np.float32).astype(ml_dtypes.bfloat16).astype(np.float64).reshape(n // 32, 32, m)
    top = np.abs(v).max(1)
    byte = np.clip(np.where(top > 0, np.frexp(top)[1] - 1 + 127 - 7, 1), 1, 254)
    codes = (v * np.exp2(127.0 - byte)[:, None, :]).reshape(n, m).astype(np.float32).astype(ml_dtypes.float8_e4m3fn).view(np.uint8)
    words = codes.reshape(n // 512, 128, 4, m).transpose(0, 1, 3, 2)
    return np.ascontiguousarray(words), np.ascontiguousarray(byte.astype(np.uint8).reshape(n // 512, 16, m))


K, T, S, N, H = 512, 2048, 512, 512, 512


def setup_inputs():
    n = np.random.standard_normal
    s = mx_kscale(K)[:, None]
    u = mx_kscale(H)
    packed_xT = pack_weight(n((K, T)) * s)
    packed_w1 = pack_fp4(n((K, H)) / np.sqrt(K) / s)
    packed_w2 = pack_fp4(n((H, N)) / np.sqrt(H) / u[:, None])
    return {
        "x_words": packed_xT[0],
        "x_scales": packed_xT[1],
        "w1_words": packed_w1[0],
        "w1_scales": packed_w1[1],
        "gn": (np.random.uniform(0.5, 1.5, (H, 1)) * u[:, None]).astype(np.float32),
        "w2_words": packed_w2[0],
        "w2_scales": packed_w2[1],
        "offs": striped8(np.random.randint(0, T, (8, S))),
        "n1": striped8(np.stack([np.random.permutation(S) for _ in range(8)])),
        "n2": striped8(np.stack([np.random.permutation(S) for _ in range(8)])),
        "n3": striped8(np.stack([np.random.permutation(S) for _ in range(8)])),
        "n4": striped8(np.stack([np.random.permutation(S) for _ in range(8)])),
        "n5": striped8(np.stack([np.random.permutation(S) for _ in range(8)])),
    }


def reference(x_words, x_scales, w1_words, w1_scales, gn, w2_words, w2_scales, offs, n1, n2, n3, n4, n5):
    xq = unpack_weight(x_words, x_scales)[np.arange(K)[:, None], runs(offs, K)]
    y = unpack_fp4(w1_words, w1_scales).T @ xq
    ex = np.exp(0.5 * y)
    z = f64(gn) * (np.log((ex + ex[np.arange(H)[:, None], runs(n1, H)]) / (ex[np.arange(H)[:, None], runs(n2, H)] + ex[np.arange(H)[:, None], runs(n3, H)])))
    h = unpack_fp4(w2_words, w2_scales).T @ mxq(z, 0, "e4m3")
    out_0 = (h[np.arange(N)[:, None], runs(n4, N)]) * (h[np.arange(N)[:, None], runs(n5, N)])
    return (out_0,) + planes(out_0)

@@ -1,0 +1,198 @@
+from contextlib import ExitStack
+
+import concourse.mybir as mybir
+
+F32 = mybir.dt.float32
+BF16 = mybir.dt.bfloat16
+U32 = mybir.dt.uint32
+I32 = mybir.dt.int32
+U16 = mybir.dt.uint16
+U8 = mybir.dt.uint8
+FP8X4 = mybir.dt.float8_e4m3fn_x4
+FP4X4 = mybir.dt.float4_e2m1fn_x4
+ACT = mybir.ActivationFunctionType
+ALU = mybir.AluOpType
+
+P = 128
+PACK = 4
+T = 2048
+S = 512
+CHUNKS = ((0, 256), (256, 384), (384, 512))
+
+FLOPS = 2 * 2 * 512 * 512 * 512
+
+
+def tile_picked_hashoddsprod_none_po_kernel(
+    tc, x_words, x_scales, w1_words, w1_scales, gn, w2_words, w2_scales, offs, n1, n2, n3, n4, n5, out_0, out_1, out_2
+):
+    nc = tc.nc
+    with ExitStack() as ctx:
+        keep = ctx.enter_context(tc.tile_pool(name="keep", bufs=1))
+        psum = ctx.enter_context(tc.psum_pool(name="psum", bufs=1))
+
+        def sb(name, shape, dtype):
+            return keep.tile(shape, dtype, name=name, align_bytes=64)
+
+        def load_list(name, src):
+            t = sb(name, [P, S // 16], U16)
+            nc.sync.dma_start(t[:], src)
+            return t
+
+        def entries(lst, c0, c1):
+            return lst[:, c0 // 16 : c1 // 16]
+
+        xs_win = sb("xs_win", [P, T], U8)
+        nc.vector.memset(xs_win[:].bitcast(I32), 0)
+        w1s_raw = sb("w1s_raw", [P, S], U8)
+        w2s_raw = sb("w2s_raw", [P, S], U8)
+        nc.gpsimd.memset(w1s_raw[:].bitcast(I32), 0)
+        nc.gpsimd.memset(w2s_raw[:].bitcast(I32), 0)
+
+        offs_t = load_list("offs_t", offs)
+        xw_win = sb("xw_win", [P, T], U32)
+        nc.sync.dma_start(xw_win[:].bitcast(I32), x_words[0].rearrange("p n t -> p (n t)").bitcast(I32))
+        xs_rows = x_scales[0].bitcast(I32)
+        for e in range(2):
+            nc.scalar.dma_start(xs_win[:].bitcast(I32)[e:P:16, :], xs_rows[e:16:2, :])
+        w1w_raw = sb("w1w_raw", [P, 2 * S], U8)
+        nc.scalar.dma_start(w1w_raw[:].bitcast(I32), w1_words[0].bitcast(I32))
+
+        def load_scale_rows(queue, dst, src):
+            rows = src[0].bitcast(I32)
+            for j in range(4):
+                queue.dma_start(dst[:].bitcast(I32)[j:P:32, :], rows[j:16:4, :])
+
+        load_scale_rows(nc.sync, w1s_raw, w1_scales)
+        load_scale_rows(nc.gpsimd, w2s_raw, w2_scales)
+        n2_t = load_list("n2_t", n2)
+        n1_t = load_list("n1_t", n1)
+        n3_t = load_list("n3_t", n3)
+
+        xs_got = sb("xs_got", [P, S], U8)
+        nc.vector.tensor_copy(xs_got[:], xs_win[:].indirect(offs_t[:]))
+        xs = sb("xs", [P, S], U8)
+        nc.vector.tensor_copy(xs[:].bitcast(I32), xs_got[:].bitcast(I32))
+        for e, queue in enumerate((nc.scalar, nc.sync)):
+            queue.dma_start(xs[:].bitcast(I32)[2 + e : P : 32, :], xs_got[:].bitcast(I32)[16 + e : P : 32, :])
+
+        def deal(name, words_raw, scales_raw, t):
+            words = sb(name + "w%d" % t, [P, 2 * P], U8)
+            scales = sb(name + "s%d" % t, [P, P], U8)
+            nc.vector.tensor_copy(
+                words[:].rearrange("p (m b) -> p m b", b=2),
+                words_raw[:].rearrange("p (m t b) -> p t m b", t=PACK, b=2)[:, t],
+            )
+            nc.vector.tensor_copy(scales[:], scales_raw[:].rearrange("p (m t) -> p t m", t=PACK)[:, t])
+            return words, scales
+
+        w1 = [deal("w1", w1w_raw, w1s_raw, 0)]
+        xw = sb("xw", [P, S], U32)
+        nc.vector.tensor_copy(xw[:], xw_win[:].indirect(offs_t[:]))
+        for t in range(1, PACK):
+            w1.append(deal("w1", w1w_raw, w1s_raw, t))
+
+        gn_t = sb("gn_t", [P, PACK], F32)
+        nc.gpsimd.dma_start(gn_t[:], gn.rearrange("(p t) o -> p (t o)", t=PACK))
+        w2w_raw = sb("w2w_raw", [P, 2 * S], U8)
+        nc.sync.dma_start(w2w_raw[:].bitcast(I32), w2_words[0].bitcast(I32))
+        n4_t = load_list("n4_t", n4)
+        n5_t = load_list("n5_t", n5)
+
+        ex, ex_plain = [], []
+        for t in range(PACK):
+            y = psum.tile([P, S], F32, name="y%d" % t)
+            nc.tensor.matmul_mx(
+                out=y[:], lhsT=w1[t][0][:].bitcast(FP4X4), lhsT_scale=w1[t][1][:],
+                rhs=xw[:].bitcast(FP8X4), rhs_scale=xs[:], start=True, stop=True,
+            )
+            ex.append(sb("ex%d" % t, [P, S], F32))
+            ex_plain.append(sb("exp%d" % t, [P, S], F32))
+            nc.scalar.activation(ex[t][:], y[:], ACT.Exp, scale=0.5)
+            nc.scalar.activation(ex_plain[t][:], y[:], ACT.Exp, scale=0.5)
+
+        w2 = [deal("w2", w2w_raw, w2s_raw, t) for t in range(PACK)]
+
+        hp = [psum.tile([P, S], F32, name="hp%d" % t) for t in range(PACK)]
+        h = [sb("h%d" % t, [P, S], F32) for t in range(PACK)]
+
+        def sums(c, t):
+            c0, c1 = CHUNKS[c]
+            w = c1 - c0
+            e2 = sb("e2_%d_%d" % (c, t), [P, w], F32)
+            nd = sb("nd_%d_%d" % (c, t), [P, 2, w], F32)
+            nc.vector.tensor_copy(e2[:], ex[t][:].indirect(entries(n2_t, c0, c1)))
+            nc.vector.tensor_tensor(nd[:, 0, :], ex[t][:].indirect(entries(n1_t, c0, c1)), ex_plain[t][:, c0:c1], ALU.add)
+            nc.vector.tensor_tensor(nd[:, 1, :], ex[t][:].indirect(entries(n3_t, c0, c1)), e2[:], ALU.add)
+            ln = sb("ln_%d_%d" % (c, t), [P, 2, w], F32)
+            nc.scalar.activation(ln[:], nd[:], ACT.Ln)
+            lg = sb("lg_%d_%d" % (c, t), [P, w], F32)
+            nc.scalar.activation(lg[:], ln[:, 1, :], ACT.Copy, scale=gn_t[:, t : t + 1])
+            return ln, lg
+
+        def z_plane(planes, t, ln, lg):
+            nc.vector.scalar_tensor_tensor(planes[:, t, :], ln[:, 0, :], gn_t[:, t : t + 1], lg[:], ALU.mult, ALU.subtract)
+
+        def second_product(c, parts):
+            c0, c1 = CHUNKS[c]
+            w = c1 - c0
+            planes = sb("zp%d" % c, [P, PACK, w], BF16)
+            for t in range(PACK):
+                z_plane(planes, t, *parts[t])
+            grouped = sb("zg%d" % c, [P, w, PACK], BF16)
+            eng_copy = nc.vector.tensor_copy if c == len(CHUNKS) - 1 else nc.scalar.copy
+            eng_copy(grouped[:], planes[:].rearrange("p t c -> p c t"))
+            codes = sb("zc%d" % c, [P, w], U32)
+            scales = sb("zs%d" % c, [P, w], U8)
+            nc.vector.quantize_mx(out=codes[:].bitcast(FP8X4), scales=scales[:], in_=grouped[:].rearrange("p c t -> p (c t)"))
+            for t in range(PACK):
+                nc.tensor.matmul_mx(
+                    out=hp[t][:, c0:c1], lhsT=w2[t][0][:].bitcast(FP4X4), lhsT_scale=w2[t][1][:],
+                    rhs=codes[:].bitcast(FP8X4), rhs_scale=scales[:], start=True, stop=True,
+                )
+                nc.scalar.copy(h[t][:, c0:c1], hp[t][:, c0:c1])
+
+        waiting = None
+        for c in range(len(CHUNKS)):
+            parts = [sums(c, t) for t in range(PACK)]
+            if waiting is not None:
+                second_product(c - 1, waiting)
+            waiting = parts
+        second_product(len(CHUNKS) - 1, waiting)
+
+        out_rows = out_0.rearrange("(p t) c -> p t c", t=PACK)
+        out_words = out_1[0].rearrange("p c t -> p (c t)").bitcast(I32)
+        o_scales = sb("o_scales", [P, S], U8)
+
+        def products(c):
+            c0, c1 = CHUNKS[c]
+            w = c1 - c0
+            o = sb("o%d" % c, [P, PACK, w], F32)
+            h4 = [sb("h4_%d_%d" % (c, t), [P, w], F32) for t in range(PACK)]
+            nc.vector.tensor_copy(h4[0][:], h[0][:].indirect(entries(n4_t, c0, c1)))
+            for t in range(PACK):
+                if t + 1 < PACK:
+                    nc.vector.tensor_copy(h4[t + 1][:], h[t + 1][:].indirect(entries(n4_t, c0, c1)))
+                nc.vector.tensor_tensor(o[:, t, :], h[t][:].indirect(entries(n5_t, c0, c1)), h4[t][:], ALU.mult)
+            nc.sync.dma_start(out_rows[:, :, c0:c1], o[:])
+            grouped = sb("og%d" % c, [P, w, PACK], BF16)
+            eng_copy = nc.vector.tensor_copy if c == len(CHUNKS) - 1 else nc.scalar.copy
+            eng_copy(grouped[:], o[:].rearrange("p t c -> p c t"))
+            return grouped
+
+        def planes_out(c, grouped):
+            c0, c1 = CHUNKS[c]
+            codes = sb("oc%d" % c, [P, c1 - c0], U32)
+            nc.vector.quantize_mx(out=codes[:].bitcast(FP8X4), scales=o_scales[:, c0:c1], in_=grouped[:].rearrange("p c t -> p (c t)"))
+            nc.sync.dma_start(out_words[:, c0:c1], codes[:].bitcast(I32))
+
+        waiting = None
+        for c in range(len(CHUNKS)):
+            grouped = products(c)
+            if waiting is not None:
+                planes_out(c - 1, waiting)
+            waiting = grouped
+        planes_out(len(CHUNKS) - 1, waiting)
+        scale_rows = out_2[0].bitcast(I32)
+        for j in range(4):
+            queue = nc.scalar if j % 2 == 0 else nc.sync
+            queue.dma_start(scale_rows[j:16:4, :], o_scales[:].bitcast(I32)[j:P:32, :])

@@ -18,6 +18,8 @@ PACK = 4
 T = 2048
 S = 512
 CHUNKS = ((0, 256), (256, 384), (384, 512))
+SCALAR_TILES = (1, 2, 3)
+SCALAR_WEAVES = ()
 
 FLOPS = 2 * 2 * 512 * 512 * 512
 
@@ -42,122 +44,148 @@ def tile_picked_hashoddsprod_none_po_kernel(
             return lst[:, c0 // 16 : c1 // 16]
 
         xs_win = sb("xs_win", [P, T], U8)
-        nc.vector.memset(xs_win[:].bitcast(I32), 0)
+        nc.gpsimd.memset(xs_win[:].bitcast(I32), 0)
         w1s_raw = sb("w1s_raw", [P, S], U8)
         w2s_raw = sb("w2s_raw", [P, S], U8)
-        nc.gpsimd.memset(w1s_raw[:].bitcast(I32), 0)
-        nc.gpsimd.memset(w2s_raw[:].bitcast(I32), 0)
+        xs = sb("xs", [P, S], U8)
+        nc.vector.memset(w1s_raw[:].bitcast(I32), 0)
+        nc.vector.memset(w2s_raw[:].bitcast(I32), 0)
+        nc.vector.memset(xs[:].bitcast(I32), 0)
 
         offs_t = load_list("offs_t", offs)
+        w1w_raw = sb("w1w_raw", [P, 2 * S], U8)
+        nc.sync.dma_start(w1w_raw[:].bitcast(I32), w1_words[0].bitcast(I32))
         xw_win = sb("xw_win", [P, T], U32)
         nc.sync.dma_start(xw_win[:].bitcast(I32), x_words[0].rearrange("p n t -> p (n t)").bitcast(I32))
         xs_rows = x_scales[0].bitcast(I32)
         for e in range(2):
             nc.scalar.dma_start(xs_win[:].bitcast(I32)[e:P:16, :], xs_rows[e:16:2, :])
-        w1w_raw = sb("w1w_raw", [P, 2 * S], U8)
-        nc.scalar.dma_start(w1w_raw[:].bitcast(I32), w1_words[0].bitcast(I32))
 
-        def load_scale_rows(queue, dst, src):
+        def load_scale_rows(queues, dst, src):
             rows = src[0].bitcast(I32)
             for j in range(4):
-                queue.dma_start(dst[:].bitcast(I32)[j:P:32, :], rows[j:16:4, :])
+                queues[j % len(queues)].dma_start(dst[:].bitcast(I32)[j:P:32, :], rows[j:16:4, :])
 
-        load_scale_rows(nc.sync, w1s_raw, w1_scales)
-        load_scale_rows(nc.gpsimd, w2s_raw, w2_scales)
+        load_scale_rows((nc.sync,), w1s_raw, w1_scales)
+        w2w_raw = sb("w2w_raw", [P, 2 * S], U8)
+        nc.sync.dma_start(w2w_raw[:].bitcast(I32), w2_words[0].bitcast(I32))
+        load_scale_rows((nc.gpsimd,), w2s_raw, w2_scales)
         n2_t = load_list("n2_t", n2)
-        n1_t = load_list("n1_t", n1)
         n3_t = load_list("n3_t", n3)
+        n1_t = load_list("n1_t", n1)
 
         xs_got = sb("xs_got", [P, S], U8)
         nc.vector.tensor_copy(xs_got[:], xs_win[:].indirect(offs_t[:]))
-        xs = sb("xs", [P, S], U8)
-        nc.vector.tensor_copy(xs[:].bitcast(I32), xs_got[:].bitcast(I32))
-        for e, queue in enumerate((nc.scalar, nc.sync)):
-            queue.dma_start(xs[:].bitcast(I32)[2 + e : P : 32, :], xs_got[:].bitcast(I32)[16 + e : P : 32, :])
+        for e in range(2):
+            nc.scalar.dma_start(xs[:].bitcast(I32)[2 + e : P : 32, :], xs_got[:].bitcast(I32)[16 + e : P : 32, :])
+        for q in range(4):
+            nc.vector.tensor_copy(xs[:].bitcast(I32)[32 * q : 32 * q + 2, :], xs_got[:].bitcast(I32)[32 * q : 32 * q + 2, :])
 
-        def deal(name, words_raw, scales_raw, t):
-            words = sb(name + "w%d" % t, [P, 2 * P], U8)
-            scales = sb(name + "s%d" % t, [P, P], U8)
-            nc.vector.tensor_copy(
-                words[:].rearrange("p (m b) -> p m b", b=2),
-                words_raw[:].rearrange("p (m t b) -> p t m b", t=PACK, b=2)[:, t],
+        def deal(eng, name, words_raw, scales_raw, t0, t1):
+            n = t1 - t0
+            words = sb(name + "w%d" % t0, [P, n, 2 * P], U8)
+            scales = sb(name + "s%d" % t0, [P, n, P], U8)
+            eng.tensor_copy(
+                words[:].rearrange("p t (m b) -> p t m b", b=2),
+                words_raw[:].rearrange("p (m t b) -> p t m b", t=PACK, b=2)[:, t0:t1],
             )
-            nc.vector.tensor_copy(scales[:], scales_raw[:].rearrange("p (m t) -> p t m", t=PACK)[:, t])
-            return words, scales
+            eng.tensor_copy(scales[:], scales_raw[:].rearrange("p (m t) -> p t m", t=PACK)[:, t0:t1])
+            return [(words[:, i, :], scales[:, i, :]) for i in range(n)]
 
-        w1 = [deal("w1", w1w_raw, w1s_raw, 0)]
+        w1 = deal(nc.vector, "w1", w1w_raw, w1s_raw, 0, 2)
         xw = sb("xw", [P, S], U32)
         nc.vector.tensor_copy(xw[:], xw_win[:].indirect(offs_t[:]))
-        for t in range(1, PACK):
-            w1.append(deal("w1", w1w_raw, w1s_raw, t))
+        w1 = w1 + deal(nc.vector, "w1", w1w_raw, w1s_raw, 2, 4)
+        w2 = deal(nc.gpsimd, "w2", w2w_raw, w2s_raw, 0, 4)
 
         gn_t = sb("gn_t", [P, PACK], F32)
-        nc.gpsimd.dma_start(gn_t[:], gn.rearrange("(p t) o -> p (t o)", t=PACK))
-        w2w_raw = sb("w2w_raw", [P, 2 * S], U8)
-        nc.sync.dma_start(w2w_raw[:].bitcast(I32), w2_words[0].bitcast(I32))
+        nc.sync.dma_start(gn_t[:], gn.rearrange("(p t) o -> p (t o)", t=PACK))
         n4_t = load_list("n4_t", n4)
         n5_t = load_list("n5_t", n5)
 
-        ex, ex_plain = [], []
+        ex, ex_plain, yp = [], [], []
         for t in range(PACK):
-            y = psum.tile([P, S], F32, name="y%d" % t)
+            yp.append(psum.tile([P, S], F32, name="y%d" % t))
             nc.tensor.matmul_mx(
-                out=y[:], lhsT=w1[t][0][:].bitcast(FP4X4), lhsT_scale=w1[t][1][:],
+                out=yp[t][:], lhsT=w1[t][0].bitcast(FP4X4), lhsT_scale=w1[t][1],
                 rhs=xw[:].bitcast(FP8X4), rhs_scale=xs[:], start=True, stop=True,
             )
             ex.append(sb("ex%d" % t, [P, S], F32))
             ex_plain.append(sb("exp%d" % t, [P, S], F32))
-            nc.scalar.activation(ex[t][:], y[:], ACT.Exp, scale=0.5)
-            nc.scalar.activation(ex_plain[t][:], y[:], ACT.Exp, scale=0.5)
+            nc.scalar.activation(ex[t][:], yp[t][:], ACT.Exp, scale=0.5)
+            nc.sync.dma_start(ex_plain[t][:], ex[t][:])
 
-        w2 = [deal("w2", w2w_raw, w2s_raw, t) for t in range(PACK)]
+        e2 = {}
+        for c, (c0, c1) in enumerate(CHUNKS):
+            for t in range(PACK):
+                e2[c, t] = sb("e2_%d_%d" % (c, t), [P, c1 - c0], F32)
+        y = {}
+        for c, (c0, c1) in enumerate(CHUNKS):
+            for t in SCALAR_TILES:
+                if c == 0:
+                    y[t] = sb("ys%d" % t, [P, S], F32)
+                    nc.scalar.copy(y[t][:], yp[t][:])
+                nc.scalar.activation(e2[c, t][:], y[t][:].indirect(entries(n2_t, c0, c1)), ACT.Exp, scale=0.5)
 
         hp = [psum.tile([P, S], F32, name="hp%d" % t) for t in range(PACK)]
         h = [sb("h%d" % t, [P, S], F32) for t in range(PACK)]
 
-        def sums(c, t):
+        def sums(c):
             c0, c1 = CHUNKS[c]
             w = c1 - c0
-            e2 = sb("e2_%d_%d" % (c, t), [P, w], F32)
-            nd = sb("nd_%d_%d" % (c, t), [P, 2, w], F32)
-            nc.vector.tensor_copy(e2[:], ex[t][:].indirect(entries(n2_t, c0, c1)))
-            nc.vector.tensor_tensor(nd[:, 0, :], ex[t][:].indirect(entries(n1_t, c0, c1)), ex_plain[t][:, c0:c1], ALU.add)
-            nc.vector.tensor_tensor(nd[:, 1, :], ex[t][:].indirect(entries(n3_t, c0, c1)), e2[:], ALU.add)
-            ln = sb("ln_%d_%d" % (c, t), [P, 2, w], F32)
-            nc.scalar.activation(ln[:], nd[:], ACT.Ln)
-            lg = sb("lg_%d_%d" % (c, t), [P, w], F32)
-            nc.scalar.activation(lg[:], ln[:, 1, :], ACT.Copy, scale=gn_t[:, t : t + 1])
-            return ln, lg
+            nd = [sb("nd_%d_%d" % (c, t), [P, 2, w], F32) for t in range(PACK)]
+            parts = []
 
-        def z_plane(planes, t, ln, lg):
-            nc.vector.scalar_tensor_tensor(planes[:, t, :], ln[:, 0, :], gn_t[:, t : t + 1], lg[:], ALU.mult, ALU.subtract)
+            def fetch(t):
+                nc.vector.tensor_copy(e2[c, t][:], ex[t][:].indirect(entries(n2_t, c0, c1)))
+
+            def num(t):
+                nc.vector.tensor_tensor(nd[t][:, 0, :], ex[t][:].indirect(entries(n1_t, c0, c1)), ex_plain[t][:, c0:c1], ALU.add)
+
+            def den(t):
+                nc.vector.tensor_tensor(nd[t][:, 1, :], ex[t][:].indirect(entries(n3_t, c0, c1)), e2[c, t][:], ALU.add)
+
+            def logs(t):
+                ln = sb("ln_%d_%d" % (c, t), [P, 2, w], F32)
+                nc.scalar.activation(ln[:], nd[t][:], ACT.Ln)
+                lg = sb("lg_%d_%d" % (c, t), [P, w], F32)
+                nc.scalar.activation(lg[:], ln[:, 1, :], ACT.Copy, scale=gn_t[:, t : t + 1])
+                parts.append((ln, lg))
+
+            mine = [t for t in range(PACK) if t not in SCALAR_TILES]
+            for t in mine:
+                fetch(t)
+            for t in mine:
+                den(t)
+            for t in range(PACK):
+                num(t)
+                if t in SCALAR_TILES:
+                    den(t)
+                logs(t)
+            return parts
 
         def second_product(c, parts):
             c0, c1 = CHUNKS[c]
             w = c1 - c0
             planes = sb("zp%d" % c, [P, PACK, w], BF16)
-            for t in range(PACK):
-                z_plane(planes, t, *parts[t])
+            for t, (ln, lg) in enumerate(parts):
+                nc.vector.scalar_tensor_tensor(planes[:, t, :], ln[:, 0, :], gn_t[:, t : t + 1], lg[:], ALU.mult, ALU.subtract)
             grouped = sb("zg%d" % c, [P, w, PACK], BF16)
-            eng_copy = nc.vector.tensor_copy if c == len(CHUNKS) - 1 else nc.scalar.copy
+            eng_copy = nc.scalar.copy if c in SCALAR_WEAVES else nc.vector.tensor_copy
             eng_copy(grouped[:], planes[:].rearrange("p t c -> p c t"))
             codes = sb("zc%d" % c, [P, w], U32)
             scales = sb("zs%d" % c, [P, w], U8)
             nc.vector.quantize_mx(out=codes[:].bitcast(FP8X4), scales=scales[:], in_=grouped[:].rearrange("p c t -> p (c t)"))
             for t in range(PACK):
                 nc.tensor.matmul_mx(
-                    out=hp[t][:, c0:c1], lhsT=w2[t][0][:].bitcast(FP4X4), lhsT_scale=w2[t][1][:],
+                    out=hp[t][:, c0:c1], lhsT=w2[t][0].bitcast(FP4X4), lhsT_scale=w2[t][1],
                     rhs=codes[:].bitcast(FP8X4), rhs_scale=scales[:], start=True, stop=True,
                 )
                 nc.scalar.copy(h[t][:, c0:c1], hp[t][:, c0:c1])
 
-        waiting = None
+        all_parts = [sums(c) for c in range(len(CHUNKS))]
         for c in range(len(CHUNKS)):
-            parts = [sums(c, t) for t in range(PACK)]
-            if waiting is not None:
-                second_product(c - 1, waiting)
-            waiting = parts
-        second_product(len(CHUNKS) - 1, waiting)
+            second_product(c, all_parts[c])
 
         out_rows = out_0.rearrange("(p t) c -> p t c", t=PACK)
         out_words = out_1[0].rearrange("p c t -> p (c t)").bitcast(I32)

@@ -17,9 +17,10 @@ P = 128
 PACK = 4
 T = 2048
 S = 512
-CHUNKS = ((0, 256), (256, 384), (384, 512))
-SCALAR_TILES = (1, 2, 3)
-SCALAR_WEAVES = ()
+HALF = S // 2
+Z_CHUNKS = ((0, 256), (256, 384), (384, 512))
+O_CHUNKS = ((0, 384), (384, 512))
+ON_VECTOR = ((0, 0), (1, 0), (0, 1))
 
 FLOPS = 2 * 2 * 512 * 512 * 512
 
@@ -30,10 +31,11 @@ def tile_picked_hashoddsprod_none_po_kernel(
     nc = tc.nc
     with ExitStack() as ctx:
         keep = ctx.enter_context(tc.tile_pool(name="keep", bufs=1))
+        shared = ctx.enter_context(tc.tile_pool(name="shared", bufs=1))
         psum = ctx.enter_context(tc.psum_pool(name="psum", bufs=1))
 
-        def sb(name, shape, dtype):
-            return keep.tile(shape, dtype, name=name, align_bytes=64)
+        def sb(name, shape, dtype, tag=None):
+            return keep.tile(shape, dtype, name=name, tag=tag or name, align_bytes=64)
 
         def load_list(name, src):
             t = sb(name, [P, S // 16], U16)
@@ -43,156 +45,149 @@ def tile_picked_hashoddsprod_none_po_kernel(
         def entries(lst, c0, c1):
             return lst[:, c0 // 16 : c1 // 16]
 
-        xs_win = sb("xs_win", [P, T], U8)
-        nc.gpsimd.memset(xs_win[:].bitcast(I32), 0)
-        w1s_raw = sb("w1s_raw", [P, S], U8)
-        w2s_raw = sb("w2s_raw", [P, S], U8)
         xs = sb("xs", [P, S], U8)
-        nc.vector.memset(w1s_raw[:].bitcast(I32), 0)
-        nc.vector.memset(w2s_raw[:].bitcast(I32), 0)
         nc.vector.memset(xs[:].bitcast(I32), 0)
 
+        def load_scale_row(queue, dst, src, j):
+            rows = src[0].bitcast(I32)[j:16:4, :]
+            queue.dma_start(dst[:].bitcast(I32)[j:P:4, :], rows.unsqueeze(1).broadcast_to([4, 8, S // 4]))
+
         offs_t = load_list("offs_t", offs)
+        xs_win = sb("xs_win", [P, T], U8)
+        nc.scalar.dma_start(xs_win[:].bitcast(I32), x_scales[0].bitcast(I32).unsqueeze(1).broadcast_to([16, 8, T // 4]))
         w1w_raw = sb("w1w_raw", [P, 2 * S], U8)
         nc.sync.dma_start(w1w_raw[:].bitcast(I32), w1_words[0].bitcast(I32))
-        xw_win = sb("xw_win", [P, T], U32)
-        nc.sync.dma_start(xw_win[:].bitcast(I32), x_words[0].rearrange("p n t -> p (n t)").bitcast(I32))
-        xs_rows = x_scales[0].bitcast(I32)
-        for e in range(2):
-            nc.scalar.dma_start(xs_win[:].bitcast(I32)[e:P:16, :], xs_rows[e:16:2, :])
-
-        def load_scale_rows(queues, dst, src):
-            rows = src[0].bitcast(I32)
-            for j in range(4):
-                queues[j % len(queues)].dma_start(dst[:].bitcast(I32)[j:P:32, :], rows[j:16:4, :])
-
-        load_scale_rows((nc.sync,), w1s_raw, w1_scales)
-        w2w_raw = sb("w2w_raw", [P, 2 * S], U8)
-        nc.sync.dma_start(w2w_raw[:].bitcast(I32), w2_words[0].bitcast(I32))
-        load_scale_rows((nc.gpsimd,), w2s_raw, w2_scales)
+        w1s_raw = sb("w1s_raw", [P, S], U8)
+        for j in range(4):
+            load_scale_row(nc.sync if j < 2 else nc.gpsimd, w1s_raw, w1_scales, j)
         n2_t = load_list("n2_t", n2)
         n3_t = load_list("n3_t", n3)
+        xw_win = shared.tile([P, T], U32, name="xw_win", offset=4 * S * PACK)
+        nc.sync.dma_start(xw_win[:].bitcast(I32), x_words[0].rearrange("p n t -> p (n t)").bitcast(I32))
         n1_t = load_list("n1_t", n1)
+        w2w_raw = sb("w2w_raw", [P, 2 * S], U8)
+        nc.gpsimd.dma_start(w2w_raw[:].bitcast(I32), w2_words[0].bitcast(I32))
+        w2s_raw = sb("w2s_raw", [P, S], U8)
+        for j in range(4):
+            load_scale_row(nc.gpsimd, w2s_raw, w2_scales, j)
+
+        def deal_words(eng, words, raw):
+            eng.tensor_copy(words[:].rearrange("p t (m b) -> p t m b", b=2), raw[:].rearrange("p (m t b) -> p t m b", t=PACK, b=2))
+            return words
+
+        def deal_scales(eng, name, raw):
+            scales = sb(name, [P, PACK, P], U8)
+            eng.tensor_copy(scales[:], raw[:].rearrange("p (m t) -> p t m", t=PACK))
+            return scales
 
         xs_got = sb("xs_got", [P, S], U8)
         nc.vector.tensor_copy(xs_got[:], xs_win[:].indirect(offs_t[:]))
-        for e in range(2):
-            nc.scalar.dma_start(xs[:].bitcast(I32)[2 + e : P : 32, :], xs_got[:].bitcast(I32)[16 + e : P : 32, :])
-        for q in range(4):
-            nc.vector.tensor_copy(xs[:].bitcast(I32)[32 * q : 32 * q + 2, :], xs_got[:].bitcast(I32)[32 * q : 32 * q + 2, :])
-
-        def deal(eng, name, words_raw, scales_raw, t0, t1):
-            n = t1 - t0
-            words = sb(name + "w%d" % t0, [P, n, 2 * P], U8)
-            scales = sb(name + "s%d" % t0, [P, n, P], U8)
-            eng.tensor_copy(
-                words[:].rearrange("p t (m b) -> p t m b", b=2),
-                words_raw[:].rearrange("p (m t b) -> p t m b", t=PACK, b=2)[:, t0:t1],
-            )
-            eng.tensor_copy(scales[:], scales_raw[:].rearrange("p (m t) -> p t m", t=PACK)[:, t0:t1])
-            return [(words[:, i, :], scales[:, i, :]) for i in range(n)]
-
-        w1 = deal(nc.vector, "w1", w1w_raw, w1s_raw, 0, 2)
+        for j in range(4):
+            queue = nc.scalar if j % 2 == 0 else nc.sync
+            queue.dma_start(xs[:].bitcast(I32)[j:P:32, :], xs_got[:].bitcast(I32)[8 * j : P : 32, :])
+        w1w = deal_words(nc.vector, sb("w1w", [P, PACK, 2 * P], U8), w1w_raw)
+        w1s = deal_scales(nc.vector, "w1s", w1s_raw)
         xw = sb("xw", [P, S], U32)
         nc.vector.tensor_copy(xw[:], xw_win[:].indirect(offs_t[:]))
-        w1 = w1 + deal(nc.vector, "w1", w1w_raw, w1s_raw, 2, 4)
-        w2 = deal(nc.gpsimd, "w2", w2w_raw, w2s_raw, 0, 4)
+        w2w = deal_words(nc.vector, shared.tile([P, PACK, 2 * P], U8, name="w2w", offset=4 * S * PACK, align_bytes=64), w2w_raw)
+        w2s = deal_scales(nc.gpsimd, "w2s", w2s_raw)
 
         gn_t = sb("gn_t", [P, PACK], F32)
-        nc.sync.dma_start(gn_t[:], gn.rearrange("(p t) o -> p (t o)", t=PACK))
+        nc.gpsimd.dma_start(gn_t[:], gn.rearrange("(p t) o -> p (t o)", t=PACK))
         n4_t = load_list("n4_t", n4)
         n5_t = load_list("n5_t", n5)
 
-        ex, ex_plain, yp = [], [], []
+        yp = [psum.tile([P, S], F32, name="yp%d" % t) for t in range(PACK)]
         for t in range(PACK):
-            yp.append(psum.tile([P, S], F32, name="y%d" % t))
             nc.tensor.matmul_mx(
-                out=yp[t][:], lhsT=w1[t][0].bitcast(FP4X4), lhsT_scale=w1[t][1],
+                out=yp[t][:], lhsT=w1w[:, t, :].bitcast(FP4X4), lhsT_scale=w1s[:, t, :],
                 rhs=xw[:].bitcast(FP8X4), rhs_scale=xs[:], start=True, stop=True,
             )
-            ex.append(sb("ex%d" % t, [P, S], F32))
-            ex_plain.append(sb("exp%d" % t, [P, S], F32))
+        ex = [sb("ex%d" % t, [P, S], F32) for t in range(PACK)]
+        ex_plain = [sb("ex_plain%d" % t, [P, S], F32) for t in range(PACK)]
+        y = [None] + [sb("y%d" % t, [P, S], F32) for t in range(1, PACK)]
+        e2_first = shared.tile([P, PACK, S], F32, name="e2_first", offset=0)
+        e2 = [[e2_first[:, t, :HALF] for t in range(PACK)], [sb("e2_second%d" % t, [P, HALF], F32)[:] for t in range(PACK)]]
+
+        def exp_out(t):
             nc.scalar.activation(ex[t][:], yp[t][:], ACT.Exp, scale=0.5)
             nc.sync.dma_start(ex_plain[t][:], ex[t][:])
 
-        e2 = {}
-        for c, (c0, c1) in enumerate(CHUNKS):
+        def y_out(t):
+            nc.scalar.copy(y[t][:], yp[t][:])
+
+        def exp_gather(u, t):
+            if (u, t) not in ON_VECTOR:
+                nc.scalar.activation(e2[u][t], y[t][:].indirect(entries(n2_t, u * HALF, (u + 1) * HALF)), ACT.Exp, scale=0.5)
+
+        for t in range(3):
+            exp_out(t)
+        y_out(2)
+        exp_out(3)
+        exp_gather(0, 2)
+        y_out(3)
+        y_out(1)
+        exp_gather(0, 3)
+        for t in range(1, PACK):
+            exp_gather(1, t)
+
+        nd = [
+            [sb("nd_first%d" % t, [P, 2, HALF], F32) for t in range(PACK)],
+            [shared.tile([P, 2, HALF], F32, name="nd_second%d" % t, offset=4 * S * t) for t in range(PACK)],
+        ]
+        for u, t in ON_VECTOR:
+            nc.vector.tensor_copy(e2[u][t], ex[t][:].indirect(entries(n2_t, u * HALF, (u + 1) * HALF)))
+        for u in range(2):
+            c0, c1 = u * HALF, (u + 1) * HALF
             for t in range(PACK):
-                e2[c, t] = sb("e2_%d_%d" % (c, t), [P, c1 - c0], F32)
-        y = {}
-        for c, (c0, c1) in enumerate(CHUNKS):
-            for t in SCALAR_TILES:
-                if c == 0:
-                    y[t] = sb("ys%d" % t, [P, S], F32)
-                    nc.scalar.copy(y[t][:], yp[t][:])
-                nc.scalar.activation(e2[c, t][:], y[t][:].indirect(entries(n2_t, c0, c1)), ACT.Exp, scale=0.5)
+                nc.vector.tensor_tensor(nd[u][t][:, 1, :], ex[t][:].indirect(entries(n3_t, c0, c1)), e2[u][t], ALU.add)
+                nc.vector.tensor_tensor(nd[u][t][:, 0, :], ex[t][:].indirect(entries(n1_t, c0, c1)), ex_plain[t][:, c0:c1], ALU.add)
 
         hp = [psum.tile([P, S], F32, name="hp%d" % t) for t in range(PACK)]
-        h = [sb("h%d" % t, [P, S], F32) for t in range(PACK)]
+        h = [shared.tile([P, S], F32, name="h%d" % t, offset=4 * S * t) for t in range(PACK)]
 
-        def sums(c):
-            c0, c1 = CHUNKS[c]
-            w = c1 - c0
-            nd = [sb("nd_%d_%d" % (c, t), [P, 2, w], F32) for t in range(PACK)]
-            parts = []
-
-            def fetch(t):
-                nc.vector.tensor_copy(e2[c, t][:], ex[t][:].indirect(entries(n2_t, c0, c1)))
-
-            def num(t):
-                nc.vector.tensor_tensor(nd[t][:, 0, :], ex[t][:].indirect(entries(n1_t, c0, c1)), ex_plain[t][:, c0:c1], ALU.add)
-
-            def den(t):
-                nc.vector.tensor_tensor(nd[t][:, 1, :], ex[t][:].indirect(entries(n3_t, c0, c1)), e2[c, t][:], ALU.add)
-
-            def logs(t):
-                ln = sb("ln_%d_%d" % (c, t), [P, 2, w], F32)
-                nc.scalar.activation(ln[:], nd[t][:], ACT.Ln)
-                lg = sb("lg_%d_%d" % (c, t), [P, w], F32)
-                nc.scalar.activation(lg[:], ln[:, 1, :], ACT.Copy, scale=gn_t[:, t : t + 1])
-                parts.append((ln, lg))
-
-            mine = [t for t in range(PACK) if t not in SCALAR_TILES]
-            for t in mine:
-                fetch(t)
-            for t in mine:
-                den(t)
+        logs = []
+        for c, (c0, c1) in enumerate(Z_CHUNKS):
+            u, w = c0 // HALF, c1 - c0
+            logs.append([])
             for t in range(PACK):
-                num(t)
-                if t in SCALAR_TILES:
-                    den(t)
-                logs(t)
-            return parts
+                ln = sb("ln_%d_%d" % (c, t), [P, 2, w], F32)
+                nc.scalar.activation(ln[:], nd[u][t][:, :, c0 - u * HALF : c1 - u * HALF], ACT.Ln)
+                lg = sb("lg_%d_%d" % (c, t), [P, w], F32)
+                logs[c].append((ln, lg))
+                if t > 0:
+                    nc.scalar.activation(logs[c][t - 1][1][:], logs[c][t - 1][0][:, 1, :], ACT.Copy, scale=gn_t[:, t - 1 : t])
+            nc.scalar.activation(lg[:], ln[:, 1, :], ACT.Copy, scale=gn_t[:, PACK - 1 : PACK])
 
-        def second_product(c, parts):
-            c0, c1 = CHUNKS[c]
+        for c, (c0, c1) in enumerate(Z_CHUNKS):
             w = c1 - c0
             planes = sb("zp%d" % c, [P, PACK, w], BF16)
-            for t, (ln, lg) in enumerate(parts):
+            for t, (ln, lg) in enumerate(logs[c]):
                 nc.vector.scalar_tensor_tensor(planes[:, t, :], ln[:, 0, :], gn_t[:, t : t + 1], lg[:], ALU.mult, ALU.subtract)
             grouped = sb("zg%d" % c, [P, w, PACK], BF16)
-            eng_copy = nc.scalar.copy if c in SCALAR_WEAVES else nc.vector.tensor_copy
-            eng_copy(grouped[:], planes[:].rearrange("p t c -> p c t"))
+            weave = nc.scalar.copy if c == 1 else nc.vector.tensor_copy
+            weave(grouped[:], planes[:].rearrange("p t c -> p c t"))
             codes = sb("zc%d" % c, [P, w], U32)
             scales = sb("zs%d" % c, [P, w], U8)
             nc.vector.quantize_mx(out=codes[:].bitcast(FP8X4), scales=scales[:], in_=grouped[:].rearrange("p c t -> p (c t)"))
+            banks = yp if c == len(Z_CHUNKS) - 1 else hp
             for t in range(PACK):
                 nc.tensor.matmul_mx(
-                    out=hp[t][:, c0:c1], lhsT=w2[t][0].bitcast(FP4X4), lhsT_scale=w2[t][1],
+                    out=banks[t][:, c0:c1], lhsT=w2w[:, t, :].bitcast(FP4X4), lhsT_scale=w2s[:, t, :],
                     rhs=codes[:].bitcast(FP8X4), rhs_scale=scales[:], start=True, stop=True,
                 )
-                nc.scalar.copy(h[t][:, c0:c1], hp[t][:, c0:c1])
-
-        all_parts = [sums(c) for c in range(len(CHUNKS))]
-        for c in range(len(CHUNKS)):
-            second_product(c, all_parts[c])
+                if c == len(Z_CHUNKS) - 2:
+                    nc.scalar.copy(h[t][:, :c1], hp[t][:, :c1])
+                if c == len(Z_CHUNKS) - 1:
+                    out_of_bank = nc.vector.tensor_copy if t == 0 else nc.scalar.copy
+                    out_of_bank(h[t][:, c0:c1], banks[t][:, c0:c1])
 
         out_rows = out_0.rearrange("(p t) c -> p t c", t=PACK)
         out_words = out_1[0].rearrange("p c t -> p (c t)").bitcast(I32)
         o_scales = sb("o_scales", [P, S], U8)
 
         def products(c):
-            c0, c1 = CHUNKS[c]
+            c0, c1 = O_CHUNKS[c]
             w = c1 - c0
             o = sb("o%d" % c, [P, PACK, w], F32)
             h4 = [sb("h4_%d_%d" % (c, t), [P, w], F32) for t in range(PACK)]
@@ -201,26 +196,33 @@ def tile_picked_hashoddsprod_none_po_kernel(
                 if t + 1 < PACK:
                     nc.vector.tensor_copy(h4[t + 1][:], h[t + 1][:].indirect(entries(n4_t, c0, c1)))
                 nc.vector.tensor_tensor(o[:, t, :], h[t][:].indirect(entries(n5_t, c0, c1)), h4[t][:], ALU.mult)
-            nc.sync.dma_start(out_rows[:, :, c0:c1], o[:])
-            grouped = sb("og%d" % c, [P, w, PACK], BF16)
-            eng_copy = nc.vector.tensor_copy if c == len(CHUNKS) - 1 else nc.scalar.copy
-            eng_copy(grouped[:], o[:].rearrange("p t c -> p c t"))
-            return grouped
+                if t % 2 == 1:
+                    nc.sync.dma_start(out_rows[:, t - 1 : t + 1, c0:c1], o[:, t - 1 : t + 1, :])
+            return o
 
-        def planes_out(c, grouped):
-            c0, c1 = CHUNKS[c]
-            codes = sb("oc%d" % c, [P, c1 - c0], U32)
-            nc.vector.quantize_mx(out=codes[:].bitcast(FP8X4), scales=o_scales[:, c0:c1], in_=grouped[:].rearrange("p c t -> p (c t)"))
-            nc.sync.dma_start(out_words[:, c0:c1], codes[:].bitcast(I32))
+        def rounded(c, o, eng_copy):
+            c0, c1 = O_CHUNKS[c]
+            pieces = []
+            for a in range(c0, c1, HALF):
+                b = min(a + HALF, c1)
+                grouped = sb("og%d" % a, [P, b - a, PACK], BF16)
+                eng_copy(grouped[:], o[:, :, a - c0 : b - c0].rearrange("p t c -> p c t"))
+                pieces.append((a, b, grouped))
+            return pieces
 
-        waiting = None
-        for c in range(len(CHUNKS)):
-            grouped = products(c)
-            if waiting is not None:
-                planes_out(c - 1, waiting)
-            waiting = grouped
-        planes_out(len(CHUNKS) - 1, waiting)
+        def planes_out(pieces):
+            for a, b, grouped in pieces:
+                codes = sb("oc%d" % a, [P, b - a], U32)
+                nc.vector.quantize_mx(out=codes[:].bitcast(FP8X4), scales=o_scales[:, a:b], in_=grouped[:].rearrange("p c t -> p (c t)"))
+                nc.scalar.dma_start(out_words[:, a:b], codes[:].bitcast(I32))
+
+        waiting = []
+        for c in range(len(O_CHUNKS)):
+            o = products(c)
+            planes_out(waiting)
+            waiting = rounded(c, o, nc.vector.tensor_copy if c == len(O_CHUNKS) - 1 else nc.scalar.copy)
+        planes_out(waiting)
         scale_rows = out_2[0].bitcast(I32)
         for j in range(4):
-            queue = nc.scalar if j % 2 == 0 else nc.sync
+            queue = nc.scalar if j % 2 == 1 else nc.sync
             queue.dma_start(scale_rows[j:16:4, :], o_scales[:].bitcast(I32)[j:P:32, :])

@@ -18,9 +18,10 @@ PACK = 4
 T = 2048
 S = 512
 HALF = S // 2
+LAST_QUARTER = S // 4
 Z_CHUNKS = ((0, 256), (256, 384), (384, 512))
 O_CHUNKS = ((0, 384), (384, 512))
-ON_VECTOR = ((0, 0), (1, 0), (0, 1))
+ON_VECTOR = ((0, 0), (1, 0))
 
 FLOPS = 2 * 2 * 512 * 512 * 512
 
@@ -88,7 +89,8 @@ def tile_picked_hashoddsprod_none_po_kernel(
         w1w = deal_words(nc.vector, sb("w1w", [P, PACK, 2 * P], U8), w1w_raw)
         w1s = deal_scales(nc.vector, "w1s", w1s_raw)
         xw = sb("xw", [P, S], U32)
-        nc.vector.tensor_copy(xw[:], xw_win[:].indirect(offs_t[:]))
+        for u in range(2):
+            nc.vector.tensor_copy(xw[:, u * HALF : (u + 1) * HALF], xw_win[:].indirect(entries(offs_t, u * HALF, (u + 1) * HALF)))
         w2w = deal_words(nc.vector, shared.tile([P, PACK, 2 * P], U8, name="w2w", offset=4 * S * PACK, align_bytes=64), w2w_raw)
         w2s = deal_scales(nc.gpsimd, "w2s", w2s_raw)
 
@@ -98,37 +100,48 @@ def tile_picked_hashoddsprod_none_po_kernel(
         n5_t = load_list("n5_t", n5)
 
         yp = [psum.tile([P, S], F32, name="yp%d" % t) for t in range(PACK)]
-        for t in range(PACK):
+        hp = [psum.tile([P, S], F32, name="hp%d" % t) for t in range(PACK)]
+
+        def first_product(bank, t, c0, c1):
             nc.tensor.matmul_mx(
-                out=yp[t][:], lhsT=w1w[:, t, :].bitcast(FP4X4), lhsT_scale=w1s[:, t, :],
-                rhs=xw[:].bitcast(FP8X4), rhs_scale=xs[:], start=True, stop=True,
+                out=bank[:, c0:c1], lhsT=w1w[:, t, :].bitcast(FP4X4), lhsT_scale=w1s[:, t, :],
+                rhs=xw[:, c0:c1].bitcast(FP8X4), rhs_scale=xs[:, c0:c1], start=True, stop=True,
             )
+
+        first_product(hp[0], 0, 0, HALF)
+        first_product(yp[0], 0, HALF, S)
+        for t in range(1, PACK):
+            first_product(yp[t], t, 0, S)
         ex = [sb("ex%d" % t, [P, S], F32) for t in range(PACK)]
         ex_plain = [sb("ex_plain%d" % t, [P, S], F32) for t in range(PACK)]
         y = [None] + [sb("y%d" % t, [P, S], F32) for t in range(1, PACK)]
-        e2_first = shared.tile([P, PACK, S], F32, name="e2_first", offset=0)
-        e2 = [[e2_first[:, t, :HALF] for t in range(PACK)], [sb("e2_second%d" % t, [P, HALF], F32)[:] for t in range(PACK)]]
+        e2_first = shared.tile([P, PACK - 1, S], F32, name="e2_first", offset=4 * S)
+        e2 = [[sb("e2_first0", [P, HALF], F32)[:]] + [e2_first[:, t - 1, :HALF] for t in range(1, PACK)], [sb("e2_second%d" % t, [P, HALF], F32)[:] for t in range(PACK)]]
 
         def exp_out(t):
-            nc.scalar.activation(ex[t][:], yp[t][:], ACT.Exp, scale=0.5)
+            if t == 0:
+                nc.scalar.activation(ex[0][:, :HALF], hp[0][:, :HALF], ACT.Exp, scale=0.5)
+                nc.scalar.activation(ex[0][:, HALF:], yp[0][:, HALF:], ACT.Exp, scale=0.5)
+            else:
+                nc.scalar.activation(ex[t][:], yp[t][:], ACT.Exp, scale=0.5)
             nc.sync.dma_start(ex_plain[t][:], ex[t][:])
 
         def y_out(t):
             nc.scalar.copy(y[t][:], yp[t][:])
 
         def exp_gather(u, t):
-            if (u, t) not in ON_VECTOR:
-                nc.scalar.activation(e2[u][t], y[t][:].indirect(entries(n2_t, u * HALF, (u + 1) * HALF)), ACT.Exp, scale=0.5)
+            w = HALF - LAST_QUARTER if (u, t) == (1, PACK - 1) else HALF
+            nc.scalar.activation(e2[u][t][:, :w], y[t][:].indirect(entries(n2_t, u * HALF, u * HALF + w)), ACT.Exp, scale=0.5)
 
-        for t in range(3):
-            exp_out(t)
-        y_out(2)
-        exp_out(3)
-        exp_gather(0, 2)
-        y_out(3)
-        y_out(1)
-        exp_gather(0, 3)
+        exp_out(0)
         for t in range(1, PACK):
+            exp_out(t)
+            if t > 1:
+                exp_gather(0, t - 1)
+            y_out(t)
+        exp_gather(1, 1)
+        exp_gather(0, PACK - 1)
+        for t in range(2, PACK):
             exp_gather(1, t)
 
         nd = [
@@ -137,13 +150,13 @@ def tile_picked_hashoddsprod_none_po_kernel(
         ]
         for u, t in ON_VECTOR:
             nc.vector.tensor_copy(e2[u][t], ex[t][:].indirect(entries(n2_t, u * HALF, (u + 1) * HALF)))
+        nc.vector.tensor_copy(e2[1][PACK - 1][:, HALF - LAST_QUARTER :], ex[PACK - 1][:].indirect(entries(n2_t, S - LAST_QUARTER, S)))
         for u in range(2):
             c0, c1 = u * HALF, (u + 1) * HALF
             for t in range(PACK):
                 nc.vector.tensor_tensor(nd[u][t][:, 1, :], ex[t][:].indirect(entries(n3_t, c0, c1)), e2[u][t], ALU.add)
                 nc.vector.tensor_tensor(nd[u][t][:, 0, :], ex[t][:].indirect(entries(n1_t, c0, c1)), ex_plain[t][:, c0:c1], ALU.add)
 
-        hp = [psum.tile([P, S], F32, name="hp%d" % t) for t in range(PACK)]
         h = [shared.tile([P, S], F32, name="h%d" % t, offset=4 * S * t) for t in range(PACK)]
 
         logs = []
@@ -165,8 +178,7 @@ def tile_picked_hashoddsprod_none_po_kernel(
             for t, (ln, lg) in enumerate(logs[c]):
                 nc.vector.scalar_tensor_tensor(planes[:, t, :], ln[:, 0, :], gn_t[:, t : t + 1], lg[:], ALU.mult, ALU.subtract)
             grouped = sb("zg%d" % c, [P, w, PACK], BF16)
-            weave = nc.scalar.copy if c == 1 else nc.vector.tensor_copy
-            weave(grouped[:], planes[:].rearrange("p t c -> p c t"))
+            nc.vector.tensor_copy(grouped[:], planes[:].rearrange("p t c -> p c t"))
             codes = sb("zc%d" % c, [P, w], U32)
             scales = sb("zs%d" % c, [P, w], U8)
             nc.vector.quantize_mx(out=codes[:].bitcast(FP8X4), scales=scales[:], in_=grouped[:].rearrange("p c t -> p (c t)"))

from contextlib import ExitStack

import concourse.mybir as mybir

F32 = mybir.dt.float32
BF16 = mybir.dt.bfloat16
U32 = mybir.dt.uint32
I32 = mybir.dt.int32
U16 = mybir.dt.uint16
U8 = mybir.dt.uint8
FP8X4 = mybir.dt.float8_e4m3fn_x4
FP4X4 = mybir.dt.float4_e2m1fn_x4
ACT = mybir.ActivationFunctionType
ALU = mybir.AluOpType

P = 128
PACK = 4
T = 2048
S = 512
HALF = S // 2
LAST_QUARTER = S // 4
Z_CHUNKS = ((0, 256), (256, 384), (384, 512))
O_CHUNKS = ((0, 384), (384, 512))
ON_VECTOR = ((0, 0), (1, 0))

FLOPS = 2 * 2 * 512 * 512 * 512


def tile_picked_hashoddsprod_none_po_kernel(
    tc, x_words, x_scales, w1_words, w1_scales, gn, w2_words, w2_scales, offs, n1, n2, n3, n4, n5, out_0, out_1, out_2
):
    nc = tc.nc
    with ExitStack() as ctx:
        keep = ctx.enter_context(tc.tile_pool(name="keep", bufs=1))
        shared = ctx.enter_context(tc.tile_pool(name="shared", bufs=1))
        psum = ctx.enter_context(tc.psum_pool(name="psum", bufs=1))

        def sb(name, shape, dtype, tag=None):
            return keep.tile(shape, dtype, name=name, tag=tag or name, align_bytes=64)

        def load_list(name, src):
            t = sb(name, [P, S // 16], U16)
            nc.sync.dma_start(t[:], src)
            return t

        def entries(lst, c0, c1):
            return lst[:, c0 // 16 : c1 // 16]

        xs = sb("xs", [P, S], U8)
        nc.vector.memset(xs[:].bitcast(I32), 0)

        def load_scale_row(queue, dst, src, j):
            rows = src[0].bitcast(I32)[j:16:4, :]
            queue.dma_start(dst[:].bitcast(I32)[j:P:4, :], rows.unsqueeze(1).broadcast_to([4, 8, S // 4]))

        offs_t = load_list("offs_t", offs)
        xs_win = sb("xs_win", [P, T], U8)
        nc.scalar.dma_start(xs_win[:].bitcast(I32), x_scales[0].bitcast(I32).unsqueeze(1).broadcast_to([16, 8, T // 4]))
        w1w_raw = sb("w1w_raw", [P, 2 * S], U8)
        nc.sync.dma_start(w1w_raw[:].bitcast(I32), w1_words[0].bitcast(I32))
        w1s_raw = sb("w1s_raw", [P, S], U8)
        for j in range(4):
            load_scale_row(nc.sync if j < 2 else nc.gpsimd, w1s_raw, w1_scales, j)
        n2_t = load_list("n2_t", n2)
        n3_t = load_list("n3_t", n3)
        xw_win = shared.tile([P, T], U32, name="xw_win", offset=4 * S * PACK)
        nc.sync.dma_start(xw_win[:].bitcast(I32), x_words[0].rearrange("p n t -> p (n t)").bitcast(I32))
        n1_t = load_list("n1_t", n1)
        w2w_raw = sb("w2w_raw", [P, 2 * S], U8)
        nc.gpsimd.dma_start(w2w_raw[:].bitcast(I32), w2_words[0].bitcast(I32))
        w2s_raw = sb("w2s_raw", [P, S], U8)
        for j in range(4):
            load_scale_row(nc.gpsimd, w2s_raw, w2_scales, j)

        def deal_words(eng, words, raw):
            eng.tensor_copy(words[:].rearrange("p t (m b) -> p t m b", b=2), raw[:].rearrange("p (m t b) -> p t m b", t=PACK, b=2))
            return words

        def deal_scales(eng, name, raw):
            scales = sb(name, [P, PACK, P], U8)
            eng.tensor_copy(scales[:], raw[:].rearrange("p (m t) -> p t m", t=PACK))
            return scales

        xs_got = sb("xs_got", [P, S], U8)
        nc.vector.tensor_copy(xs_got[:], xs_win[:].indirect(offs_t[:]))
        for j in range(4):
            queue = nc.scalar if j % 2 == 0 else nc.sync
            queue.dma_start(xs[:].bitcast(I32)[j:P:32, :], xs_got[:].bitcast(I32)[8 * j : P : 32, :])
        w1w = deal_words(nc.vector, sb("w1w", [P, PACK, 2 * P], U8), w1w_raw)
        w1s = deal_scales(nc.vector, "w1s", w1s_raw)
        xw = sb("xw", [P, S], U32)
        for u in range(2):
            nc.vector.tensor_copy(xw[:, u * HALF : (u + 1) * HALF], xw_win[:].indirect(entries(offs_t, u * HALF, (u + 1) * HALF)))
        w2w = deal_words(nc.vector, shared.tile([P, PACK, 2 * P], U8, name="w2w", offset=4 * S * PACK, align_bytes=64), w2w_raw)
        w2s = deal_scales(nc.gpsimd, "w2s", w2s_raw)

        gn_t = sb("gn_t", [P, PACK], F32)
        nc.gpsimd.dma_start(gn_t[:], gn.rearrange("(p t) o -> p (t o)", t=PACK))
        n4_t = load_list("n4_t", n4)
        n5_t = load_list("n5_t", n5)

        yp = [psum.tile([P, S], F32, name="yp%d" % t) for t in range(PACK)]
        hp = [psum.tile([P, S], F32, name="hp%d" % t) for t in range(PACK)]

        def first_product(bank, t, c0, c1):
            nc.tensor.matmul_mx(
                out=bank[:, c0:c1], lhsT=w1w[:, t, :].bitcast(FP4X4), lhsT_scale=w1s[:, t, :],
                rhs=xw[:, c0:c1].bitcast(FP8X4), rhs_scale=xs[:, c0:c1], start=True, stop=True,
            )

        first_product(hp[0], 0, 0, HALF)
        first_product(yp[0], 0, HALF, S)
        for t in range(1, PACK):
            first_product(yp[t], t, 0, S)
        ex = [sb("ex%d" % t, [P, S], F32) for t in range(PACK)]
        ex_plain = [sb("ex_plain%d" % t, [P, S], F32) for t in range(PACK)]
        y = [None] + [sb("y%d" % t, [P, S], F32) for t in range(1, PACK)]
        e2_first = shared.tile([P, PACK - 1, S], F32, name="e2_first", offset=4 * S)
        e2 = [[sb("e2_first0", [P, HALF], F32)[:]] + [e2_first[:, t - 1, :HALF] for t in range(1, PACK)], [sb("e2_second%d" % t, [P, HALF], F32)[:] for t in range(PACK)]]

        def exp_out(t):
            if t == 0:
                nc.scalar.activation(ex[0][:, :HALF], hp[0][:, :HALF], ACT.Exp, scale=0.5)
                nc.scalar.activation(ex[0][:, HALF:], yp[0][:, HALF:], ACT.Exp, scale=0.5)
            else:
                nc.scalar.activation(ex[t][:], yp[t][:], ACT.Exp, scale=0.5)
            nc.sync.dma_start(ex_plain[t][:], ex[t][:])

        def y_out(t):
            nc.scalar.copy(y[t][:], yp[t][:])

        def exp_gather(u, t):
            w = HALF - LAST_QUARTER if (u, t) == (1, PACK - 1) else HALF
            nc.scalar.activation(e2[u][t][:, :w], y[t][:].indirect(entries(n2_t, u * HALF, u * HALF + w)), ACT.Exp, scale=0.5)

        exp_out(0)
        for t in range(1, PACK):
            exp_out(t)
            if t > 1:
                exp_gather(0, t - 1)
            y_out(t)
        exp_gather(1, 1)
        exp_gather(0, PACK - 1)
        for t in range(2, PACK):
            exp_gather(1, t)

        nd = [
            [sb("nd_first%d" % t, [P, 2, HALF], F32) for t in range(PACK)],
            [shared.tile([P, 2, HALF], F32, name="nd_second%d" % t, offset=4 * S * t) for t in range(PACK)],
        ]
        for u, t in ON_VECTOR:
            nc.vector.tensor_copy(e2[u][t], ex[t][:].indirect(entries(n2_t, u * HALF, (u + 1) * HALF)))
        nc.vector.tensor_copy(e2[1][PACK - 1][:, HALF - LAST_QUARTER :], ex[PACK - 1][:].indirect(entries(n2_t, S - LAST_QUARTER, S)))
        for u in range(2):
            c0, c1 = u * HALF, (u + 1) * HALF
            for t in range(PACK):
                nc.vector.tensor_tensor(nd[u][t][:, 1, :], ex[t][:].indirect(entries(n3_t, c0, c1)), e2[u][t], ALU.add)
                nc.vector.tensor_tensor(nd[u][t][:, 0, :], ex[t][:].indirect(entries(n1_t, c0, c1)), ex_plain[t][:, c0:c1], ALU.add)

        h = [shared.tile([P, S], F32, name="h%d" % t, offset=4 * S * t) for t in range(PACK)]

        logs = []
        for c, (c0, c1) in enumerate(Z_CHUNKS):
            u, w = c0 // HALF, c1 - c0
            logs.append([])
            for t in range(PACK):
                ln = sb("ln_%d_%d" % (c, t), [P, 2, w], F32)
                nc.scalar.activation(ln[:], nd[u][t][:, :, c0 - u * HALF : c1 - u * HALF], ACT.Ln)
                lg = sb("lg_%d_%d" % (c, t), [P, w], F32)
                logs[c].append((ln, lg))
                if t > 0:
                    nc.scalar.activation(logs[c][t - 1][1][:], logs[c][t - 1][0][:, 1, :], ACT.Copy, scale=gn_t[:, t - 1 : t])
            nc.scalar.activation(lg[:], ln[:, 1, :], ACT.Copy, scale=gn_t[:, PACK - 1 : PACK])

        for c, (c0, c1) in enumerate(Z_CHUNKS):
            w = c1 - c0
            planes = sb("zp%d" % c, [P, PACK, w], BF16)
            for t, (ln, lg) in enumerate(logs[c]):
                nc.vector.scalar_tensor_tensor(planes[:, t, :], ln[:, 0, :], gn_t[:, t : t + 1], lg[:], ALU.mult, ALU.subtract)
            grouped = sb("zg%d" % c, [P, w, PACK], BF16)
            nc.vector.tensor_copy(grouped[:], planes[:].rearrange("p t c -> p c t"))
            codes = sb("zc%d" % c, [P, w], U32)
            scales = sb("zs%d" % c, [P, w], U8)
            nc.vector.quantize_mx(out=codes[:].bitcast(FP8X4), scales=scales[:], in_=grouped[:].rearrange("p c t -> p (c t)"))
            banks = yp if c == len(Z_CHUNKS) - 1 else hp
            for t in range(PACK):
                nc.tensor.matmul_mx(
                    out=banks[t][:, c0:c1], lhsT=w2w[:, t, :].bitcast(FP4X4), lhsT_scale=w2s[:, t, :],
                    rhs=codes[:].bitcast(FP8X4), rhs_scale=scales[:], start=True, stop=True,
                )
                if c == len(Z_CHUNKS) - 2:
                    nc.scalar.copy(h[t][:, :c1], hp[t][:, :c1])
                if c == len(Z_CHUNKS) - 1:
                    out_of_bank = nc.vector.tensor_copy if t == 0 else nc.scalar.copy
                    out_of_bank(h[t][:, c0:c1], banks[t][:, c0:c1])

        out_rows = out_0.rearrange("(p t) c -> p t c", t=PACK)
        out_words = out_1[0].rearrange("p c t -> p (c t)").bitcast(I32)
        o_scales = sb("o_scales", [P, S], U8)

        def products(c):
            c0, c1 = O_CHUNKS[c]
            w = c1 - c0
            o = sb("o%d" % c, [P, PACK, w], F32)
            h4 = [sb("h4_%d_%d" % (c, t), [P, w], F32) for t in range(PACK)]
            nc.vector.tensor_copy(h4[0][:], h[0][:].indirect(entries(n4_t, c0, c1)))
            for t in range(PACK):
                if t + 1 < PACK:
                    nc.vector.tensor_copy(h4[t + 1][:], h[t + 1][:].indirect(entries(n4_t, c0, c1)))
                nc.vector.tensor_tensor(o[:, t, :], h[t][:].indirect(entries(n5_t, c0, c1)), h4[t][:], ALU.mult)
                if t % 2 == 1:
                    nc.sync.dma_start(out_rows[:, t - 1 : t + 1, c0:c1], o[:, t - 1 : t + 1, :])
            return o

        def rounded(c, o, eng_copy):
            c0, c1 = O_CHUNKS[c]
            pieces = []
            for a in range(c0, c1, HALF):
                b = min(a + HALF, c1)
                grouped = sb("og%d" % a, [P, b - a, PACK], BF16)
                eng_copy(grouped[:], o[:, :, a - c0 : b - c0].rearrange("p t c -> p c t"))
                pieces.append((a, b, grouped))
            return pieces

        def planes_out(pieces):
            for a, b, grouped in pieces:
                codes = sb("oc%d" % a, [P, b - a], U32)
                nc.vector.quantize_mx(out=codes[:].bitcast(FP8X4), scales=o_scales[:, a:b], in_=grouped[:].rearrange("p c t -> p (c t)"))
                nc.scalar.dma_start(out_words[:, a:b], codes[:].bitcast(I32))

        waiting = []
        for c in range(len(O_CHUNKS)):
            o = products(c)
            planes_out(waiting)
            waiting = rounded(c, o, nc.vector.tensor_copy if c == len(O_CHUNKS) - 1 else nc.scalar.copy)
        planes_out(waiting)
        scale_rows = out_2[0].bitcast(I32)
        for j in range(4):
            queue = nc.scalar if j % 2 == 1 else nc.sync
            queue.dma_start(scale_rows[j:16:4, :], o_scales[:].bitcast(I32)[j:P:32, :])
